import numpy as np
CORES = [40,41,42,43,44,45,46,47,80,81,82,83,84,85,86,87]
N = 16
WIDTHS = [28,112,56,14,56,224,56,0,112,14,112,112,56,28,14,14]
OFF = [0,28,140,196,210,266,490,546,546,658,672,784,896,952,980,994]
C = 1008
def setup_inputs(rng):
    return {"x": rng.standard_normal((N, 128, C), dtype=np.float32)}
def reference(x):
    s = x.sum(axis=0, dtype=np.float64).astype(x.dtype)
    YW = max(WIDTHS)
    y = np.full((N, 128, YW), np.nan, x.dtype)
    for r in range(N):
        y[r][:, :WIDTHS[r]] = s[:, OFF[r]:OFF[r] + WIDTHS[r]]
    return {"y": y}

@@ -1,0 +1,112 @@
+from concourse.bass import DstId, RemoteDMATransfer
+from concourse.mybir import AluOpType
+import comms_topo
+
+SLOT = 144
+SCRATCH = {
+    "xs": ("sbuf", [128, 1008], "float32"),
+    "land": ("sbuf", [128, 7 * SLOT], "float32"),
+    "fa": ("sbuf", [128, 224], "float32"),
+    "fb": ("sbuf", [128, 224], "float32"),
+}
+SEMAPHORES = ["loaded", "arr", "sent", "fa_in", "fb_in", "stored", "added"]
+
+
+def _cut(a, b, n):
+    return [(a + (b - a) * i // n, a + (b - a) * (i + 1) // n) for i in range(n)]
+
+
+def _perms(items):
+    if len(items) <= 1:
+        return [list(items)]
+    out = []
+    for i in range(len(items)):
+        for rest in _perms(items[:i] + items[i + 1:]):
+            out.append([items[i]] + rest)
+    return out
+
+
+def make_plan(cores, widths, off, ncols):
+    owner_span = {c: (off[r], off[r] + widths[r]) for r, c in enumerate(cores)}
+    chips = sorted({comms_topo.chip(c) for c in cores})
+    ranges = {}
+    for ch in chips:
+        mine = [c for c in cores if comms_topo.chip(c) == ch]
+        far = [c for c in cores if comms_topo.chip(c) != ch]
+        lo = min(owner_span[c][0] for c in mine)
+        hi = max(owner_span[c][1] for c in mine)
+        flo = min(owner_span[c][0] for c in far)
+        fhi = max(owner_span[c][1] for c in far)
+        gates = [c for c in mine if comms_topo.may_write(c, far[0])]
+        inner = [c for c in mine if c not in gates]
+        for c, r in zip(gates, _cut(flo, fhi, len(gates))):
+            ranges[c] = r
+        parts = _cut(lo, hi, len(inner))
+        for order in _perms(inner):
+            if all(min(p[1], owner_span[c][1]) <= max(p[0], owner_span[c][0]) for c, p in zip(order, parts)):
+                for c, p in zip(order, parts):
+                    ranges[c] = p
+                break
+    pieces = {}
+    for c in cores:
+        a, b = ranges[c]
+        pieces[c] = []
+        for o in cores:
+            s, e = max(a, owner_span[o][0]), min(b, owner_span[o][1])
+            if e > s:
+                pieces[c].append((s, e - s, o, owner_span[o][0]))
+    return ranges, pieces
+
+
+def _bits(m):
+    return bin(m).count("1")
+
+
+def rank_program(g, core, T, topo):
+    rank = T.rank_of(core)
+    if rank is None:
+        return
+    cores = list(T.cores)
+    widths, off, ncols = T.tables["WIDTHS"], T.tables["OFF"], T.tables["C"]
+    ranges, pieces = make_plan(cores, widths, off, ncols)
+    chipmates = [c for c in cores if topo.chip(c) == topo.chip(core)]
+    others = [c for c in chipmates if c != core]
+    sent = 0
+
+    g.sync.dma_start(T.xs[:], T.x[:]).then_inc(T.sem.loaded, 16)
+    g.wait_ge(T.sem.loaded, 16)
+
+    for d in others:
+        a, b = ranges[d]
+        slot = [c for c in chipmates if c != d].index(core)
+        rid, pid, _ = topo.addr(d)
+        m = topo.mask(core, d)
+        g.remote_dma(T.land[:, slot * SLOT:slot * SLOT + (b - a)], T.xs[:, a:b], T.sem.arr, T.sem.sent, pid, rid, m)
+        sent += _bits(m)
+
+    g.wait_ge(T.sem.arr, 16 * len(others))
+    a0 = ranges[core][0]
+    for (a, w, o, ofirst) in pieces[core]:
+        near = topo.chip(o) == topo.chip(core)
+        rid, pid, _ = topo.addr(o)
+        m = topo.mask(core, o)
+        srcs = [T.land[:, s * SLOT + a - a0:s * SLOT + a - a0 + w] for s in range(len(others))] + [T.xs[:, a:a + w]]
+        dst = (T.fa if near else T.fb)[:, a - ofirst:a - ofirst + w]
+        g.remote_dma_fused([RemoteDMATransfer(dst_ids=[DstId(rid=rid, pnc=pid)], dma_engine_mask=m,
+                                              remote_sem=T.sem.fa_in if near else T.sem.fb_in,
+                                              srcs=srcs, dsts=[dst], alu_op=1)], local_sem=T.sem.sent)
+        sent += _bits(m)
+
+    w = widths[rank]
+    if w:
+        na = sum(_bits(topo.mask(c, core)) for c in cores for p in pieces[c]
+                 if p[2] == core and topo.chip(c) == topo.chip(core))
+        nb = sum(_bits(topo.mask(c, core)) for c in cores for p in pieces[c]
+                 if p[2] == core and topo.chip(c) != topo.chip(core))
+        g.sync.wait_ge(T.sem.fa_in, na)
+        g.sync.dma_start(T.y[:, 0:w], T.fa[:, 0:w]).then_inc(T.sem.stored, 16)
+        g.wait_ge(T.sem.stored, 16)
+        g.wait_ge(T.sem.fb_in, nb)
+        g.dma_start(T.y[:, 0:w], T.fb[:, 0:w], accum_op=AluOpType.add).then_inc(T.sem.added, 16)
+        g.wait_ge(T.sem.added, 16)
+    g.wait_ge(T.sem.sent, sent)

@@ -2,7 +2,26 @@ from concourse.bass import DstId, RemoteDMATransfer
 from concourse.mybir import AluOpType
 import comms_topo
 
-SLOT = 144
+REDUCES = [
+    (210, 364),
+    (364, 490),
+    (658, 784),
+    (490, 658),
+    (0, 140),
+    (140, 210),
+    (784, 896),
+    (896, 1008),
+    (952, 1008),
+    (812, 952),
+    (0, 140),
+    (266, 399),
+    (546, 672),
+    (672, 812),
+    (140, 266),
+    (399, 546),
+]
+SLOT = max(b - a for a, b in REDUCES)
+
 SCRATCH = {
     "xs": ("sbuf", [128, 1008], "float32"),
     "land": ("sbuf", [128, 7 * SLOT], "float32"),
@@ -12,54 +31,49 @@ SCRATCH = {
 SEMAPHORES = ["loaded", "arr", "sent", "fa_in", "fb_in", "stored", "added"]
 
 
-def _cut(a, b, n):
-    return [(a + (b - a) * i // n, a + (b - a) * (i + 1) // n) for i in range(n)]
-
-
-def _perms(items):
-    if len(items) <= 1:
-        return [list(items)]
-    out = []
-    for i in range(len(items)):
-        for rest in _perms(items[:i] + items[i + 1:]):
-            out.append([items[i]] + rest)
-    return out
-
-
-def make_plan(cores, widths, off, ncols):
-    owner_span = {c: (off[r], off[r] + widths[r]) for r, c in enumerate(cores)}
-    chips = sorted({comms_topo.chip(c) for c in cores})
-    ranges = {}
-    for ch in chips:
-        mine = [c for c in cores if comms_topo.chip(c) == ch]
-        far = [c for c in cores if comms_topo.chip(c) != ch]
-        lo = min(owner_span[c][0] for c in mine)
-        hi = max(owner_span[c][1] for c in mine)
-        flo = min(owner_span[c][0] for c in far)
-        fhi = max(owner_span[c][1] for c in far)
-        gates = [c for c in mine if comms_topo.may_write(c, far[0])]
-        inner = [c for c in mine if c not in gates]
-        for c, r in zip(gates, _cut(flo, fhi, len(gates))):
-            ranges[c] = r
-        parts = _cut(lo, hi, len(inner))
-        for order in _perms(inner):
-            if all(min(p[1], owner_span[c][1]) <= max(p[0], owner_span[c][0]) for c, p in zip(order, parts)):
-                for c, p in zip(order, parts):
-                    ranges[c] = p
-                break
-    pieces = {}
-    for c in cores:
-        a, b = ranges[c]
-        pieces[c] = []
-        for o in cores:
-            s, e = max(a, owner_span[o][0]), min(b, owner_span[o][1])
-            if e > s:
-                pieces[c].append((s, e - s, o, owner_span[o][0]))
-    return ranges, pieces
-
-
 def _bits(m):
     return bin(m).count("1")
+
+
+def _calls(items):
+    left = list(items)
+    calls = []
+    while left:
+        first = left.pop(0)
+        mate = [it for it in left if it[0] == first[0]][:1]
+        if not mate:
+            calls.append([(first, 0x00FF if first[1] else 0xFFFF)])
+            continue
+        left.remove(mate[0])
+        if first[1] and mate[0][1]:
+            masks = (0x000F, 0x00F0)
+        elif mate[0][1]:
+            masks = (0xFF00, 0x00FF)
+        else:
+            masks = (0x00FF, 0xFF00)
+        calls.append([(first, masks[0]), (mate[0], masks[1])])
+    return calls
+
+
+def make_plan(cores, widths, off):
+    chip = comms_topo.chip
+    spread, folds = {}, {}
+    for r, c in enumerate(cores):
+        near = [d for d in cores if chip(d) == chip(c) and d != c]
+        far = [d for d in cores if chip(d) != chip(c)]
+        near.sort(key=lambda d: not comms_topo.may_write(d, far[0]))
+        spread[c] = _calls([(REDUCES[cores.index(d)][1] - REDUCES[cores.index(d)][0], False, d,
+                             REDUCES[cores.index(d)][0]) for d in near])
+        a, b = REDUCES[r]
+        items = []
+        for q, o in enumerate(cores):
+            s, e = max(a, off[q]), min(b, off[q] + widths[q])
+            if e > s:
+                assert o != c and comms_topo.may_write(c, o)
+                items.append((e - s, chip(o) != chip(c), o, s, s - off[q]))
+        items.sort(key=lambda it: not it[1])
+        folds[c] = _calls(items)
+    return spread, folds
 
 
 def rank_program(g, core, T, topo):
@@ -67,46 +81,46 @@ def rank_program(g, core, T, topo):
     if rank is None:
         return
     cores = list(T.cores)
-    widths, off, ncols = T.tables["WIDTHS"], T.tables["OFF"], T.tables["C"]
-    ranges, pieces = make_plan(cores, widths, off, ncols)
-    chipmates = [c for c in cores if topo.chip(c) == topo.chip(core)]
-    others = [c for c in chipmates if c != core]
+    widths, off = T.tables["WIDTHS"], T.tables["OFF"]
+    spread, folds = make_plan(cores, widths, off)
+    on_chip = [c for c in cores if topo.chip(c) == topo.chip(core)]
     sent = 0
+
+    def dst_id(c):
+        rid, pid, _ = topo.addr(c)
+        return DstId(rid=rid, pnc=pid)
 
     g.sync.dma_start(T.xs[:], T.x[:]).then_inc(T.sem.loaded, 16)
     g.wait_ge(T.sem.loaded, 16)
 
-    for d in others:
-        a, b = ranges[d]
-        slot = [c for c in chipmates if c != d].index(core)
-        rid, pid, _ = topo.addr(d)
-        m = topo.mask(core, d)
-        g.remote_dma(T.land[:, slot * SLOT:slot * SLOT + (b - a)], T.xs[:, a:b], T.sem.arr, T.sem.sent, pid, rid, m)
-        sent += _bits(m)
+    for call in spread[core]:
+        trs = []
+        for (w, _, d, a), m in call:
+            s = [c for c in on_chip if c != d].index(core) * SLOT
+            trs.append(RemoteDMATransfer(dst_ids=[dst_id(d)], dma_engine_mask=m, remote_sem=T.sem.arr,
+                                         src=T.xs[:, a:a + w], dst=T.land[:, s:s + w]))
+            sent += _bits(m)
+        g.remote_dma_fused(trs, local_sem=T.sem.sent)
 
-    g.wait_ge(T.sem.arr, 16 * len(others))
-    a0 = ranges[core][0]
-    for (a, w, o, ofirst) in pieces[core]:
-        near = topo.chip(o) == topo.chip(core)
-        rid, pid, _ = topo.addr(o)
-        m = topo.mask(core, o)
-        srcs = [T.land[:, s * SLOT + a - a0:s * SLOT + a - a0 + w] for s in range(len(others))] + [T.xs[:, a:a + w]]
-        dst = (T.fa if near else T.fb)[:, a - ofirst:a - ofirst + w]
-        g.remote_dma_fused([RemoteDMATransfer(dst_ids=[DstId(rid=rid, pnc=pid)], dma_engine_mask=m,
-                                              remote_sem=T.sem.fa_in if near else T.sem.fb_in,
-                                              srcs=srcs, dsts=[dst], alu_op=1)], local_sem=T.sem.sent)
-        sent += _bits(m)
+    g.wait_ge(T.sem.arr, sum(_bits(m) for c in on_chip for call in spread[c] for it, m in call if it[2] == core))
+    a0 = REDUCES[rank][0]
+    for call in folds[core]:
+        trs = []
+        for (w, leaves, o, a, at), m in call:
+            srcs = [T.land[:, s * SLOT + a - a0:s * SLOT + a - a0 + w] for s in range(7)] + [T.xs[:, a:a + w]]
+            trs.append(RemoteDMATransfer(dst_ids=[dst_id(o)], dma_engine_mask=m,
+                                         remote_sem=T.sem.fb_in if leaves else T.sem.fa_in,
+                                         srcs=srcs, dsts=[(T.fb if leaves else T.fa)[:, at:at + w]], alu_op=1))
+            sent += _bits(m)
+        g.remote_dma_fused(trs, local_sem=T.sem.sent)
 
     w = widths[rank]
     if w:
-        na = sum(_bits(topo.mask(c, core)) for c in cores for p in pieces[c]
-                 if p[2] == core and topo.chip(c) == topo.chip(core))
-        nb = sum(_bits(topo.mask(c, core)) for c in cores for p in pieces[c]
-                 if p[2] == core and topo.chip(c) != topo.chip(core))
-        g.sync.wait_ge(T.sem.fa_in, na)
+        mine = [(it, m) for c in cores for call in folds[c] for it, m in call if it[2] == core]
+        g.sync.wait_ge(T.sem.fa_in, sum(_bits(m) for it, m in mine if not it[1]))
         g.sync.dma_start(T.y[:, 0:w], T.fa[:, 0:w]).then_inc(T.sem.stored, 16)
         g.wait_ge(T.sem.stored, 16)
-        g.wait_ge(T.sem.fb_in, nb)
+        g.wait_ge(T.sem.fb_in, sum(_bits(m) for it, m in mine if it[1]))
         g.dma_start(T.y[:, 0:w], T.fb[:, 0:w], accum_op=AluOpType.add).then_inc(T.sem.added, 16)
         g.wait_ge(T.sem.added, 16)
     g.wait_ge(T.sem.sent, sent)

from concourse.bass import DstId, RemoteDMATransfer
from concourse.mybir import AluOpType
import comms_topo

REDUCES = [
    (210, 364),
    (364, 490),
    (658, 784),
    (490, 658),
    (0, 140),
    (140, 210),
    (784, 896),
    (896, 1008),
    (952, 1008),
    (812, 952),
    (0, 140),
    (266, 399),
    (546, 672),
    (672, 812),
    (140, 266),
    (399, 546),
]
SLOT = max(b - a for a, b in REDUCES)

SCRATCH = {
    "xs": ("sbuf", [128, 1008], "float32"),
    "land": ("sbuf", [128, 7 * SLOT], "float32"),
    "fa": ("sbuf", [128, 224], "float32"),
    "fb": ("sbuf", [128, 224], "float32"),
}
SEMAPHORES = ["loaded", "arr", "sent", "fa_in", "fb_in", "stored", "added"]


def _bits(m):
    return bin(m).count("1")


def _calls(items):
    left = list(items)
    calls = []
    while left:
        first = left.pop(0)
        mate = [it for it in left if it[0] == first[0]][:1]
        if not mate:
            calls.append([(first, 0x00FF if first[1] else 0xFFFF)])
            continue
        left.remove(mate[0])
        if first[1] and mate[0][1]:
            masks = (0x000F, 0x00F0)
        elif mate[0][1]:
            masks = (0xFF00, 0x00FF)
        else:
            masks = (0x00FF, 0xFF00)
        calls.append([(first, masks[0]), (mate[0], masks[1])])
    return calls


def make_plan(cores, widths, off):
    chip = comms_topo.chip
    spread, folds = {}, {}
    for r, c in enumerate(cores):
        near = [d for d in cores if chip(d) == chip(c) and d != c]
        far = [d for d in cores if chip(d) != chip(c)]
        near.sort(key=lambda d: not comms_topo.may_write(d, far[0]))
        spread[c] = _calls([(REDUCES[cores.index(d)][1] - REDUCES[cores.index(d)][0], False, d,
                             REDUCES[cores.index(d)][0]) for d in near])
        a, b = REDUCES[r]
        items = []
        for q, o in enumerate(cores):
            s, e = max(a, off[q]), min(b, off[q] + widths[q])
            if e > s:
                assert o != c and comms_topo.may_write(c, o)
                items.append((e - s, chip(o) != chip(c), o, s, s - off[q]))
        items.sort(key=lambda it: not it[1])
        folds[c] = _calls(items)
    return spread, folds


def rank_program(g, core, T, topo):
    rank = T.rank_of(core)
    if rank is None:
        return
    cores = list(T.cores)
    widths, off = T.tables["WIDTHS"], T.tables["OFF"]
    spread, folds = make_plan(cores, widths, off)
    on_chip = [c for c in cores if topo.chip(c) == topo.chip(core)]
    sent = 0

    def dst_id(c):
        rid, pid, _ = topo.addr(c)
        return DstId(rid=rid, pnc=pid)

    g.sync.dma_start(T.xs[:], T.x[:]).then_inc(T.sem.loaded, 16)
    g.wait_ge(T.sem.loaded, 16)

    for call in spread[core]:
        trs = []
        for (w, _, d, a), m in call:
            s = [c for c in on_chip if c != d].index(core) * SLOT
            trs.append(RemoteDMATransfer(dst_ids=[dst_id(d)], dma_engine_mask=m, remote_sem=T.sem.arr,
                                         src=T.xs[:, a:a + w], dst=T.land[:, s:s + w]))
            sent += _bits(m)
        g.remote_dma_fused(trs, local_sem=T.sem.sent)

    g.wait_ge(T.sem.arr, sum(_bits(m) for c in on_chip for call in spread[c] for it, m in call if it[2] == core))
    a0 = REDUCES[rank][0]
    for call in folds[core]:
        trs = []
        for (w, leaves, o, a, at), m in call:
            srcs = [T.land[:, s * SLOT + a - a0:s * SLOT + a - a0 + w] for s in range(7)] + [T.xs[:, a:a + w]]
            trs.append(RemoteDMATransfer(dst_ids=[dst_id(o)], dma_engine_mask=m,
                                         remote_sem=T.sem.fb_in if leaves else T.sem.fa_in,
                                         srcs=srcs, dsts=[(T.fb if leaves else T.fa)[:, at:at + w]], alu_op=1))
            sent += _bits(m)
        g.remote_dma_fused(trs, local_sem=T.sem.sent)

    w = widths[rank]
    if w:
        mine = [(it, m) for c in cores for call in folds[c] for it, m in call if it[2] == core]
        g.sync.wait_ge(T.sem.fa_in, sum(_bits(m) for it, m in mine if not it[1]))
        g.sync.dma_start(T.y[:, 0:w], T.fa[:, 0:w]).then_inc(T.sem.stored, 16)
        g.wait_ge(T.sem.stored, 16)
        g.wait_ge(T.sem.fb_in, sum(_bits(m) for it, m in mine if it[1]))
        g.dma_start(T.y[:, 0:w], T.fb[:, 0:w], accum_op=AluOpType.add).then_inc(T.sem.added, 16)
        g.wait_ge(T.sem.added, 16)
    g.wait_ge(T.sem.sent, sent)
